import numpy as np
import ml_dtypes


def mxq(x, axis, fmt="e4m3"):
    dtype, down = {"e4m3": (ml_dtypes.float8_e4m3fn, 7), "e5m2": (ml_dtypes.float8_e5m2, 14)}[fmt]
    v = np.moveaxis(np.asarray(x, np.float32).astype(ml_dtypes.bfloat16).astype(np.float64), axis, -1)
    blocks = v.reshape(v.shape[:-1] + (-1, 32))
    amax = np.abs(blocks).max(-1, keepdims=True)
    byte = np.maximum(np.where(amax > 0, np.frexp(amax)[1] - 1 + 127, 0) - down, 1)
    scale = np.exp2(byte - 127.0)
    codes = (blocks / scale).astype(np.float32).astype(dtype).astype(np.float64)
    return np.moveaxis((codes * scale).reshape(v.shape), -1, axis)


WIDE = False


def mx_kscale(k):
    if not WIDE:
        return np.ones(k)
    levels = np.array([10, -10, 5, -5, 0])
    if k % 512:
        return np.exp2(np.random.permutation(np.resize(levels, k // 32))).repeat(32)
    a = np.empty((k // 512, 16))
    for p in range(k // 512):
        a[p, :8] = np.random.permutation(np.resize(levels, 8))
        for g in range(8):
            far = levels[np.abs(levels - a[p, g]) >= 10]
            a[p, g + 8] = far[np.random.randint(len(far))]
    return np.exp2(a.ravel()).repeat(32)


def f64(x):
    return np.asarray(x).astype(np.float64)


def striped(idx):
    return np.tile(idx.reshape(-1, 16).T, (8, 1)).astype(np.uint16)


def unstriped(offs):
    return offs[:16].T.reshape(-1).astype(np.int64)


K, T, D, V, H, N = 2048, 1024, 6, 512, 1024, 128
P = 2 ** 7


def setup_inputs():
    n = np.random.standard_normal
    s = mx_kscale(K)[:, None]
    u = mx_kscale(H)
    return {
        "xT": (n((K, T)) * s).astype(np.float32),
        "w1": (n((K, H)) / np.sqrt(K) / s * u).astype(np.float32),
        "w2": (n((H, N)) / np.sqrt(H) / u[:, None]).astype(np.float32),
        "gate": np.tile(np.random.uniform(0.2, 1.0, (D, 1, V)) / np.sqrt(D), (1, P, 1)).astype(np.float32),
        "pos1": striped(np.random.permutation(T)[:V]),
        "pos2": striped(np.random.permutation(T)[:V]),
        "pos3": striped(np.random.permutation(T)[:V]),
        "pos4": striped(np.random.permutation(T)[:V]),
        "pos5": striped(np.random.permutation(T)[:V]),
        "pos6": striped(np.random.permutation(T)[:V]),
    }


def reference(xT, w1, w2, gate, pos1, pos2, pos3, pos4, pos5, pos6):
    h = mxq(f64(w1), 0, "e4m3").T @ mxq(f64(xT), 0, "e4m3")
    z = sum(f64(gate)[d, :1] * h[:, unstriped(p)] for d, p in enumerate((pos1, pos2, pos3, pos4, pos5, pos6)))
    return mxq(f64(w2), 0, "e4m3").T @ mxq(z, 0, "e4m3")

@@ -1,0 +1,343 @@
+from contextlib import ExitStack
+
+import concourse.mybir as mybir
+from concourse.masks import make_identity
+
+K, T, D, V, H, N = 2048, 1024, 6, 512, 1024, 128
+FLOPS = 2 * K * T * H + 2 * H * V * N
+
+F32 = mybir.dt.float32
+BF16 = mybir.dt.bfloat16
+U32 = mybir.dt.uint32
+U16 = mybir.dt.uint16
+U8 = mybir.dt.uint8
+X4 = mybir.dt.float8_e4m3fn_x4
+MULT = mybir.AluOpType.mult
+
+P = 128
+PASSES = K // 512
+BLOCKS = H // P
+VT = V // P
+
+
+def tile_picked_gcn_mlp_none_sub_l_kernel(tc, xT, w1, w2, gate, pos1, pos2, pos3, pos4, pos5, pos6, out):
+    nc = tc.nc
+    with ExitStack() as ctx:
+        lists_pool = ctx.enter_context(tc.tile_pool(name="lists", bufs=1))
+        keep = ctx.enter_context(tc.tile_pool(name="keep", bufs=1))
+        raw = ctx.enter_context(tc.tile_pool(name="raw", bufs=3))
+        ring = ctx.enter_context(tc.tile_pool(name="ring", bufs=4))
+        two = ctx.enter_context(tc.tile_pool(name="two", bufs=2))
+        wpool = ctx.enter_context(tc.tile_pool(name="wpool", bufs=8))
+        hbank = ctx.enter_context(tc.psum_pool(name="hbank", bufs=4))
+        zbank = ctx.enter_context(tc.psum_pool(name="zbank", bufs=2))
+
+        lists = []
+        for d in range(D):
+            offs = lists_pool.tile([P, V // 16], U16, name=f"pos_{d}")
+            lists.append(offs)
+
+        gate_rows = keep.tile([P, V], F32)
+        nc.vector.memset(gate_rows[:], 0.0)
+        ident = keep.tile([P, P], F32)
+        make_identity(nc, ident[:])
+
+        x_raw = []
+        for c in range(PASSES):
+            rows = xT[512 * c : 512 * (c + 1), :]
+            if c < PASSES - 1:
+                xr = raw.tile([P, 4, T], F32)
+                nc.sync.dma_start(out=xr[:], in_=rows.rearrange("(p j) t -> p j t", j=4))
+                x_raw.append([(xr, 0)])
+            else:
+                parts = []
+                for half in range(2):
+                    xh = raw.tile([P, 4, T // 2], F32, name="half_raw")
+                    nc.sync.dma_start(out=xh[:], in_=rows[:, 512 * half : 512 * (half + 1)].rearrange("(p j) t -> p j t", j=4))
+                    parts.append((xh, 512 * half))
+                x_raw.append(parts)
+            if c == 0:
+                nc.sync.dma_start(out=gate_rows[0:D, :], in_=gate[:, 0, :])
+            if c == 1:
+                for offs, src in zip(lists, (pos1, pos2, pos3, pos4, pos5, pos6)):
+                    nc.sync.dma_start(out=offs[:], in_=src)
+
+        w_raw = {}
+
+        def load_w1(b):
+            for c in range(PASSES):
+                wr = wpool.tile([P, 4, P], F32)
+                nc.sync.dma_start(
+                    out=wr[:],
+                    in_=w1[512 * c : 512 * (c + 1), P * b : P * (b + 1)].rearrange("(p j) w -> p j w", j=4),
+                )
+                w_raw[b, c] = wr
+
+        load_w1(0)
+        load_w1(1)
+
+        x_codes = keep.tile([P, PASSES, T], U32, align_bytes=64)
+        x_scales = keep.tile([P, PASSES, T], U8, align_bytes=64)
+
+        def prepare_x(c, lo, n, on_scalar):
+            for tile, base in x_raw[c]:
+                if base <= lo < base + tile.shape[2]:
+                    src = tile[:, :, lo - base : lo - base + n]
+            grouped = ring.tile([P, 512, 4], BF16, align_bytes=64, name="x_grouped")
+            view = grouped[:, 0:n, :]
+            copy = nc.scalar.copy if on_scalar else nc.vector.tensor_copy
+            copy(out=view, in_=src.rearrange("p j t -> p t j"))
+            nc.vector.quantize_mx(
+                out=x_codes[:, c, lo : lo + n].bitcast(X4),
+                scales=x_scales[:, c, lo : lo + n],
+                in_=view.rearrange("p t j -> p (t j)"),
+            )
+
+        prepare_x(0, 0, 512, False)
+        prepare_x(0, 512, 512, True)
+
+        gate_cols = zbank.tile([P, VT, P], F32, tag="zz")
+        for v in range(VT):
+            nc.tensor.transpose(gate_cols[:, v, :], gate_rows[:, P * v : P * (v + 1)], ident[:])
+        gate_t = keep.tile([P, VT, 8], F32)
+        nc.vector.tensor_copy(out=gate_t[:, :, 0:D], in_=gate_cols[:, :, 0:D])
+        gates = []
+        for d in range(D):
+            gb = zbank.tile([P, V], F32, tag="zt")
+            for v in range(VT):
+                nc.tensor.transpose(gb[:, P * v : P * (v + 1)], gate_t[:, v, d : d + 1].to_broadcast([P, P]), ident[:])
+            gd = keep.tile([P, V], F32, name=f"gate_{d}")
+            if d % 2 == 0:
+                nc.scalar.copy(out=gd[:], in_=gb[:])
+            else:
+                nc.vector.tensor_copy(out=gd[:], in_=gb[:])
+            gates.append(gd)
+
+        for c in range(1, PASSES - 1):
+            prepare_x(c, 0, 512, False)
+            prepare_x(c, 512, 512, True)
+        prepare_x(PASSES - 1, 256, 256, False)
+        prepare_x(PASSES - 1, 0, 256, True)
+        prepare_x(PASSES - 1, 512, 512, False)
+
+        w_codes = {}
+
+        def prepare_w1(b, c, on_scalar):
+            if c == 0:
+                codes = ring.tile([P, PASSES, P], U32, align_bytes=64, name="w_codes")
+                scales = ring.tile([P, PASSES, P], U8, align_bytes=64, name="w_scales")
+                w_codes[b] = (codes, scales)
+            codes, scales = w_codes[b]
+            grouped = wpool.tile([P, P, 4], BF16, align_bytes=64, name="w_grouped")
+            copy = nc.scalar.copy if on_scalar else nc.vector.tensor_copy
+            copy(out=grouped[:], in_=w_raw[b, c][:].rearrange("p j w -> p w j"))
+            nc.vector.quantize_mx(
+                out=codes[:, c, :].bitcast(X4), scales=scales[:, c, :], in_=grouped[:].rearrange("p w j -> p (w j)")
+            )
+
+        w_wide = {}
+
+        def load_w1_wide(b):
+            wr = raw.tile([P, PASSES, 4, P], F32, name="half_raw")
+            for c in range(PASSES):
+                nc.sync.dma_start(
+                    out=wr[:, c, :, :],
+                    in_=w1[512 * c : 512 * (c + 1), P * b : P * (b + 1)].rearrange("(p j) w -> p j w", j=4),
+                )
+            grouped = two.tile([P, PASSES, P, 4], BF16, align_bytes=64, name="w_wide_grouped")
+            nc.scalar.copy(out=grouped[:], in_=wr[:].rearrange("p c j w -> p c w j"))
+            w_wide[b] = grouped
+
+        def quantize_w1_wide(b):
+            codes = ring.tile([P, PASSES, P], U32, align_bytes=64, name="w_codes")
+            scales = ring.tile([P, PASSES, P], U8, align_bytes=64, name="w_scales")
+            w_codes[b] = (codes, scales)
+            nc.vector.quantize_mx(
+                out=codes[:].rearrange("p c w -> p (c w)").bitcast(X4),
+                scales=scales[:].rearrange("p c w -> p (c w)"),
+                in_=w_wide[b][:].rearrange("p c w j -> p (c w j)"),
+            )
+
+        h_tiles = {}
+        h_banks = {}
+
+        def project(b, c):
+            if c == 0:
+                lo = hbank.tile([P, 512], F32, name="h")
+                hi = hbank.tile([P, 512], F32, name="h")
+                h_banks[b] = (lo, hi)
+            codes, scales = w_codes[b]
+            for half in range(2):
+                cols = slice(512 * half, 512 * (half + 1))
+                nc.tensor.matmul_mx(
+                    out=h_banks[b][half][:],
+                    lhsT=codes[:, c, :].bitcast(X4),
+                    lhsT_scale=scales[:, c, :],
+                    rhs=x_codes[:, c, cols].bitcast(X4),
+                    rhs_scale=x_scales[:, c, cols],
+                    start=(c == 0),
+                    stop=(c == PASSES - 1),
+                )
+
+        def bring_out(b):
+            h = raw.tile([P, T], F32, name="h_rows")
+            h_tiles[b] = h
+            lo, hi = h_banks[b]
+            nc.scalar.copy(out=h[:, 0:512], in_=lo[:])
+            if b == 0:
+                nc.vector.tensor_copy(out=h[:, 512:1024], in_=hi[:])
+            else:
+                nc.scalar.copy(out=h[:, 512:1024], in_=hi[:])
+
+        def gather(b, d, lo, n):
+            prod = two.tile([P, V], F32, name=f"prod_{d}")
+            cols = slice(lo, lo + n)
+            if n == V:
+                offs = lists[d][:]
+            else:
+                offs = lists[d][:, lo // 16 : (lo + n) // 16]
+            nc.vector.tensor_tensor(prod[:, 0:n], h_tiles[b][:].indirect(offs), gates[d][:, cols], MULT)
+            return prod
+
+        def add_transposed(bank_cols, prod_cols, d):
+            nc.tensor.matmul(bank_cols, lhsT=prod_cols, rhs=ident[:], is_transpose=True, start=(d == 0), stop=(d == D - 1))
+
+        z_half = {}
+
+        def z_rows(b):
+            if b // 4 not in z_half:
+                zb = two.tile([P, VT, 512], BF16, align_bytes=64, name="z_rows")
+                z_half[b // 4] = zb
+            return z_half[b // 4]
+
+        def sum_block(b, prods):
+            zt = zbank.tile([P, VT, P], F32, tag="zt")
+            for v in range(VT):
+                for d in range(D):
+                    add_transposed(zt[:, v, :], prods[d][:, P * v : P * (v + 1)], d)
+            q = b % 4
+            nc.scalar.copy(out=z_rows(b)[:, :, P * q : P * (q + 1)], in_=zt[:])
+
+        z_codes = keep.tile([P, 2, V], U32, align_bytes=64)
+        z_scales = keep.tile([P, 2, V], U8, align_bytes=64)
+
+        def turn_back(half, v0, nv, grouped, copy):
+            words = z_half[half][:].rearrange("p v i -> p (v i)").bitcast(F32)
+            zz = zbank.tile([P, 2, 2, P], F32, tag="zz")
+            for v in range(nv):
+                for u in range(2):
+                    base = 256 * (v0 + v)
+                    nc.tensor.transpose(zz[:, v, u, :], words[:, base + u : base + 256 : 2], ident[:])
+            copy(
+                out=grouped.rearrange("p (v n) w -> p v n w", v=nv),
+                in_=zz[:, 0:nv, :, :].rearrange("p v u n -> p v n u"),
+            )
+
+        def quantize_z(half, v0, nv, grouped_bf):
+            cols = slice(P * v0, P * (v0 + nv))
+            nc.vector.quantize_mx(
+                out=z_codes[:, half, cols].bitcast(X4),
+                scales=z_scales[:, half, cols],
+                in_=grouped_bf,
+            )
+
+        w2_state = {}
+
+        def load_w2():
+            wr = keep.tile([P, 2, 4, P], F32, name="w2_raw")
+            for g in range(2):
+                nc.sync.dma_start(out=wr[:, g, :, :], in_=w2[512 * g : 512 * (g + 1), :].rearrange("(p j) m -> p j m", j=4))
+            grouped = keep.tile([P, 2, P, 4], BF16, align_bytes=64, name="w2_grouped")
+            nc.scalar.copy(out=grouped[:], in_=wr[:].rearrange("p g j m -> p g m j"))
+            w2_state["grouped"] = grouped
+
+        w2_codes = keep.tile([P, 2, P], U32, align_bytes=64)
+        w2_scales = keep.tile([P, 2, P], U8, align_bytes=64)
+
+        def quantize_w2():
+            nc.vector.quantize_mx(
+                out=w2_codes[:].rearrange("p g m -> p (g m)").bitcast(X4),
+                scales=w2_scales[:].rearrange("p g m -> p (g m)"),
+                in_=w2_state["grouped"][:].rearrange("p g m j -> p (g m j)"),
+            )
+
+        for c in range(PASSES):
+            prepare_w1(0, c, False)
+            project(0, c)
+        bring_out(0)
+        grouped_half = {}
+        last_prods = None
+        for b in range(BLOCKS - 1):
+            prods = []
+            for d in range(D):
+                prods.append(gather(b, d, 0, V))
+                if b == 0:
+                    if d < PASSES:
+                        prepare_w1(1, d, True)
+                        project(1, d)
+                    if d == PASSES:
+                        bring_out(1)
+                    if d == 5:
+                        load_w1_wide(2)
+                else:
+                    if d == 0:
+                        sum_block(b - 1, last_prods)
+                    if d == 1:
+                        quantize_w1_wide(b + 1)
+                        for c in range(PASSES):
+                            project(b + 1, c)
+                        bring_out(b + 1)
+                    if d == 2:
+                        if b == 1:
+                            load_w2()
+                        if b + 2 < BLOCKS:
+                            load_w1_wide(b + 2)
+                    if d == 4:
+                        if b == 2:
+                            quantize_w2()
+                        if b == 4:
+                            grouped = keep.tile([P, V, 4], BF16, align_bytes=64, name="z_grouped_0")
+                            for v0 in (0, 2):
+                                turn_back(0, v0, 2, grouped[:, P * v0 : P * (v0 + 2), :].bitcast(F32), nc.scalar.copy)
+                            grouped_half[0] = grouped
+                    if d == 0 and b == 5:
+                        quantize_z(0, 0, VT, grouped_half[0][:].rearrange("p n j -> p (n j)"))
+            last_prods = prods
+
+        b = BLOCKS - 1
+        grouped = keep.tile([P, V, 4], BF16, align_bytes=64, name="z_grouped_1")
+        zb = z_rows(b)
+        for lo, n in ((0, 384), (384, 128)):
+            v0, nv = lo // P, n // P
+            zts = []
+            for v in range(nv):
+                zt = hbank.tile([P, P], F32, name="h")
+                zts.append(zt)
+            for d in range(D):
+                prod = gather(b, d, lo, n)
+                for v in range(nv):
+                    add_transposed(zts[v][:], prod[:, P * v : P * (v + 1)], d)
+                if lo == 0 and d == 0:
+                    sum_block(b - 1, last_prods)
+            for v in range(nv):
+                copy = nc.scalar.copy if lo == 0 else nc.vector.tensor_copy
+                copy(out=zb[:, v0 + v, 384:512], in_=zts[v][:])
+            for v in range(0, nv, 2):
+                turn_back(1, v0 + v, min(2, nv - v), grouped[:, P * (v0 + v) : P * (v0 + min(v + 2, nv)), :].bitcast(F32), nc.scalar.copy)
+            acc = zbank.tile([P, n], F32, tag="zt")
+            for start, width in ((0, 256), (256, 128)) if lo == 0 else ((384, 128),):
+                cols = slice(start, start + width)
+                quantize_z(1, start // P, width // P, grouped[:, cols, :].rearrange("p n j -> p (n j)"))
+                for g in range(2):
+                    nc.tensor.matmul_mx(
+                        out=acc[:, start - lo : start - lo + width],
+                        lhsT=w2_codes[:, g, :].bitcast(X4),
+                        lhsT_scale=w2_scales[:, g, :],
+                        rhs=z_codes[:, g, cols].bitcast(X4),
+                        rhs_scale=z_scales[:, g, cols],
+                        start=(g == 0),
+                        stop=(g == 1),
+                    )
+            res = two.tile([P, 384], F32, name="result")
+            nc.scalar.copy(out=res[:, 0:n], in_=acc[:])
+            nc.sync.dma_start(out=out[:, lo : lo + n], in_=res[:, 0:n])

@@ -42,26 +42,6 @@ def tile_picked_gcn_mlp_none_sub_l_kernel(tc, xT, w1, w2, gate, pos1, pos2, pos3
         ident = keep.tile([P, P], F32)
         make_identity(nc, ident[:])
 
-        x_raw = []
-        for c in range(PASSES):
-            rows = xT[512 * c : 512 * (c + 1), :]
-            if c < PASSES - 1:
-                xr = raw.tile([P, 4, T], F32)
-                nc.sync.dma_start(out=xr[:], in_=rows.rearrange("(p j) t -> p j t", j=4))
-                x_raw.append([(xr, 0)])
-            else:
-                parts = []
-                for half in range(2):
-                    xh = raw.tile([P, 4, T // 2], F32, name="half_raw")
-                    nc.sync.dma_start(out=xh[:], in_=rows[:, 512 * half : 512 * (half + 1)].rearrange("(p j) t -> p j t", j=4))
-                    parts.append((xh, 512 * half))
-                x_raw.append(parts)
-            if c == 0:
-                nc.sync.dma_start(out=gate_rows[0:D, :], in_=gate[:, 0, :])
-            if c == 1:
-                for offs, src in zip(lists, (pos1, pos2, pos3, pos4, pos5, pos6)):
-                    nc.sync.dma_start(out=offs[:], in_=src)
-
         w_raw = {}
 
         def load_w1(b):
@@ -74,51 +54,26 @@ def tile_picked_gcn_mlp_none_sub_l_kernel(tc, xT, w1, w2, gate, pos1, pos2, pos3
                 w_raw[b, c] = wr
 
         load_w1(0)
-        load_w1(1)
-
-        x_codes = keep.tile([P, PASSES, T], U32, align_bytes=64)
-        x_scales = keep.tile([P, PASSES, T], U8, align_bytes=64)
-
-        def prepare_x(c, lo, n, on_scalar):
-            for tile, base in x_raw[c]:
-                if base <= lo < base + tile.shape[2]:
-                    src = tile[:, :, lo - base : lo - base + n]
-            grouped = ring.tile([P, 512, 4], BF16, align_bytes=64, name="x_grouped")
-            view = grouped[:, 0:n, :]
-            copy = nc.scalar.copy if on_scalar else nc.vector.tensor_copy
-            copy(out=view, in_=src.rearrange("p j t -> p t j"))
-            nc.vector.quantize_mx(
-                out=x_codes[:, c, lo : lo + n].bitcast(X4),
-                scales=x_scales[:, c, lo : lo + n],
-                in_=view.rearrange("p t j -> p (t j)"),
-            )
-
-        prepare_x(0, 0, 512, False)
-        prepare_x(0, 512, 512, True)
-
-        gate_cols = zbank.tile([P, VT, P], F32, tag="zz")
-        for v in range(VT):
-            nc.tensor.transpose(gate_cols[:, v, :], gate_rows[:, P * v : P * (v + 1)], ident[:])
-        gate_t = keep.tile([P, VT, 8], F32)
-        nc.vector.tensor_copy(out=gate_t[:, :, 0:D], in_=gate_cols[:, :, 0:D])
-        gates = []
-        for d in range(D):
-            gb = zbank.tile([P, V], F32, tag="zt")
-            for v in range(VT):
-                nc.tensor.transpose(gb[:, P * v : P * (v + 1)], gate_t[:, v, d : d + 1].to_broadcast([P, P]), ident[:])
-            gd = keep.tile([P, V], F32, name=f"gate_{d}")
-            if d % 2 == 0:
-                nc.scalar.copy(out=gd[:], in_=gb[:])
+        nc.sync.dma_start(out=gate_rows[0:D, :], in_=gate[:, 0, :])
+        x_raw = []
+        for c in range(PASSES):
+            rows = xT[512 * c : 512 * (c + 1), :]
+            if c < PASSES - 1:
+                xr = raw.tile([P, 4, T], F32)
+                nc.sync.dma_start(out=xr[:], in_=rows.rearrange("(p j) t -> p j t", j=4))
+                x_raw.append([(xr, 0)])
             else:
-                nc.vector.tensor_copy(out=gd[:], in_=gb[:])
-            gates.append(gd)
+                parts = []
+                for lo, n in ((0, 512), (512, 256), (768, 256)):
+                    xh = raw.tile([P, 4, n], F32, name="half_raw")
+                    nc.sync.dma_start(out=xh[:], in_=rows[:, lo : lo + n].rearrange("(p j) t -> p j t", j=4))
+                    parts.append((xh, lo))
+                x_raw.append(parts)
+            if c == 1:
+                for offs, src in zip(lists, (pos1, pos2, pos3, pos4, pos5, pos6)):
+                    nc.sync.dma_start(out=offs[:], in_=src)
 
-        for c in range(1, PASSES - 1):
-            prepare_x(c, 0, 512, False)
-            prepare_x(c, 512, 512, True)
-        prepare_x(PASSES - 1, 256, 256, False)
-        prepare_x(PASSES - 1, 0, 256, True)
-        prepare_x(PASSES - 1, 512, 512, False)
+        load_w1(1)
 
         w_codes = {}
 
@@ -161,33 +116,106 @@ def tile_picked_gcn_mlp_none_sub_l_kernel(tc, xT, w1, w2, gate, pos1, pos2, pos3
         h_tiles = {}
         h_banks = {}
 
+        def project_group(b, c, bank, lo, n):
+            codes, scales = w_codes[b]
+            nc.tensor.matmul_mx(
+                out=bank[:],
+                lhsT=codes[:, c, :].bitcast(X4),
+                lhsT_scale=scales[:, c, :],
+                rhs=x_codes[:, c, lo : lo + n].bitcast(X4),
+                rhs_scale=x_scales[:, c, lo : lo + n],
+                start=(c == 0),
+                stop=(c == PASSES - 1),
+            )
+
         def project(b, c):
             if c == 0:
-                lo = hbank.tile([P, 512], F32, name="h")
-                hi = hbank.tile([P, 512], F32, name="h")
-                h_banks[b] = (lo, hi)
-            codes, scales = w_codes[b]
-            for half in range(2):
-                cols = slice(512 * half, 512 * (half + 1))
-                nc.tensor.matmul_mx(
-                    out=h_banks[b][half][:],
-                    lhsT=codes[:, c, :].bitcast(X4),
-                    lhsT_scale=scales[:, c, :],
-                    rhs=x_codes[:, c, cols].bitcast(X4),
-                    rhs_scale=x_scales[:, c, cols],
-                    start=(c == 0),
-                    stop=(c == PASSES - 1),
-                )
+                h_banks[b] = []
+                for lo, n in ((0, 512), (512, 256), (768, 256)) if b == 0 else ((0, 512), (512, 512)):
+                    bank = hbank.tile([P, n], F32, name="h")
+                    h_banks[b].append((bank, lo, n))
+            for bank, lo, n in h_banks[b]:
+                if b > 0 or c < PASSES - 1 or lo < 768:
+                    project_group(b, c, bank, lo, n)
+
+        def project_last_quarter():
+            bank, lo, n = h_banks[0][2]
+            project_group(0, PASSES - 1, bank, lo, n)
+
+        x_codes = keep.tile([P, PASSES, T], U32, align_bytes=64)
+        x_scales = keep.tile([P, PASSES, T], U8, align_bytes=64)
+
+        x_grouped = {}
+
+        def interleave_x(c, lo, n, on_scalar):
+            for tile, base in x_raw[c]:
+                if base <= lo < base + tile.shape[2]:
+                    src = tile[:, :, lo - base : lo - base + n]
+            grouped = ring.tile([P, 512, 4], BF16, align_bytes=64, name="x_grouped")
+            view = grouped[:, 0:n, :]
+            copy = nc.scalar.copy if on_scalar else nc.vector.tensor_copy
+            copy(out=view, in_=src.rearrange("p j t -> p t j"))
+            x_grouped[c, lo] = view
+
+        def quantize_x(c, lo, n):
+            nc.vector.quantize_mx(
+                out=x_codes[:, c, lo : lo + n].bitcast(X4),
+                scales=x_scales[:, c, lo : lo + n],
+                in_=x_grouped[c, lo].rearrange("p t j -> p (t j)"),
+            )
+
+        def prepare_x(c, lo, n, on_scalar):
+            interleave_x(c, lo, n, on_scalar)
+            quantize_x(c, lo, n)
+
+        for c in range(PASSES):
+            prepare_w1(0, c, False)
+        gate_cols = zbank.tile([P, VT, P], F32, tag="zz")
+        for v in range(VT):
+            nc.tensor.transpose(gate_cols[:, v, :], gate_rows[:, P * v : P * (v + 1)], ident[:])
+        gate_t = keep.tile([P, VT, 8], F32)
+        nc.vector.tensor_copy(out=gate_t[:, :, 0:D], in_=gate_cols[:, :, 0:D])
+        gates = []
+        for d in range(D):
+            gb = zbank.tile([P, V], F32, tag=("zt", "zz")[d % 2])
+            for v in range(VT):
+                nc.tensor.transpose(gb[:, P * v : P * (v + 1)], gate_t[:, v, d : d + 1].to_broadcast([P, P]), ident[:])
+            gd = keep.tile([P, V], F32, name=f"gate_{d}")
+            if d % 2 == 0:
+                nc.scalar.copy(out=gd[:], in_=gb[:])
+            else:
+                nc.vector.tensor_copy(out=gd[:], in_=gb[:])
+            gates.append(gd)
+
+        for c in range(3):
+            interleave_x(c, 512, 512, True)
+            prepare_x(c, 0, 512, False)
+            if c > 0:
+                quantize_x(c - 1, 512, 512)
+                project(0, c - 1)
+        interleave_x(3, 0, 256, True)
+        prepare_x(3, 256, 256, False)
+        quantize_x(2, 512, 512)
+        project(0, 2)
+        prepare_x(3, 512, 256, False)
+        quantize_x(3, 0, 256)
+        project(0, 3)
+        first = raw.tile([P, T], F32, name="h_rows")
+        h_tiles[0] = first
+        nc.scalar.copy(out=first[:, 0:512], in_=h_banks[0][0][0][:])
+        interleave_x(3, 768, 128, False)
+        interleave_x(3, 896, 128, True)
+        nc.vector.tensor_copy(out=first[:, 512:768], in_=h_banks[0][1][0][:])
+        quantize_x(3, 768, 128)
+        quantize_x(3, 896, 128)
+        project_last_quarter()
+        nc.scalar.copy(out=first[:, 768:1024], in_=h_banks[0][2][0][:])
 
         def bring_out(b):
             h = raw.tile([P, T], F32, name="h_rows")
             h_tiles[b] = h
-            lo, hi = h_banks[b]
-            nc.scalar.copy(out=h[:, 0:512], in_=lo[:])
-            if b == 0:
-                nc.vector.tensor_copy(out=h[:, 512:1024], in_=hi[:])
-            else:
-                nc.scalar.copy(out=h[:, 512:1024], in_=hi[:])
+            for bank, lo, n in h_banks[b]:
+                nc.scalar.copy(out=h[:, lo : lo + n], in_=bank[:])
 
         def gather(b, d, lo, n):
             prod = two.tile([P, V], F32, name=f"prod_{d}")
@@ -261,10 +289,6 @@ def tile_picked_gcn_mlp_none_sub_l_kernel(tc, xT, w1, w2, gate, pos1, pos2, pos3
                 in_=w2_state["grouped"][:].rearrange("p g m j -> p (g m j)"),
             )
 
-        for c in range(PASSES):
-            prepare_w1(0, c, False)
-            project(0, c)
-        bring_out(0)
         grouped_half = {}
         last_prods = None
         for b in range(BLOCKS - 1):
@@ -307,23 +331,28 @@ def tile_picked_gcn_mlp_none_sub_l_kernel(tc, xT, w1, w2, gate, pos1, pos2, pos3
         b = BLOCKS - 1
         grouped = keep.tile([P, V, 4], BF16, align_bytes=64, name="z_grouped_1")
         zb = z_rows(b)
+        zts = []
+        for v in range(VT):
+            zt = hbank.tile([P, P], F32, name="h")
+            zts.append(zt)
+        for d in range(3):
+            prod = gather(b, d, 0, V)
+            for v in range(VT):
+                add_transposed(zts[v][:], prod[:, P * v : P * (v + 1)], d)
+            if d == 0:
+                sum_block(b - 1, last_prods)
         for lo, n in ((0, 384), (384, 128)):
             v0, nv = lo // P, n // P
-            zts = []
-            for v in range(nv):
-                zt = hbank.tile([P, P], F32, name="h")
-                zts.append(zt)
-            for d in range(D):
+            for d in range(3, D):
                 prod = gather(b, d, lo, n)
                 for v in range(nv):
-                    add_transposed(zts[v][:], prod[:, P * v : P * (v + 1)], d)
-                if lo == 0 and d == 0:
-                    sum_block(b - 1, last_prods)
-            for v in range(nv):
+                    add_transposed(zts[v0 + v][:], prod[:, P * v : P * (v + 1)], d)
+            for v in range(v0, v0 + nv):
                 copy = nc.scalar.copy if lo == 0 else nc.vector.tensor_copy
-                copy(out=zb[:, v0 + v, 384:512], in_=zts[v][:])
+                copy(out=zb[:, v, 384:512], in_=zts[v][:])
             for v in range(0, nv, 2):
                 turn_back(1, v0 + v, min(2, nv - v), grouped[:, P * (v0 + v) : P * (v0 + min(v + 2, nv)), :].bitcast(F32), nc.scalar.copy)
+        for lo, n in ((0, 384), (384, 128)):
             acc = zbank.tile([P, n], F32, tag="zt")
             for start, width in ((0, 256), (256, 128)) if lo == 0 else ((384, 128),):
                 cols = slice(start, start + width)

@@ -74,6 +74,7 @@ def tile_picked_gcn_mlp_none_sub_l_kernel(tc, xT, w1, w2, gate, pos1, pos2, pos3
                     nc.sync.dma_start(out=offs[:], in_=src)
 
         load_w1(1)
+        load_w1(2)
 
         w_codes = {}
 
@@ -92,6 +93,8 @@ def tile_picked_gcn_mlp_none_sub_l_kernel(tc, xT, w1, w2, gate, pos1, pos2, pos3
 
         w_wide = {}
 
+        w_wide_raw = {}
+
         def load_w1_wide(b):
             wr = raw.tile([P, PASSES, 4, P], F32, name="half_raw")
             for c in range(PASSES):
@@ -99,8 +102,11 @@ def tile_picked_gcn_mlp_none_sub_l_kernel(tc, xT, w1, w2, gate, pos1, pos2, pos3
                     out=wr[:, c, :, :],
                     in_=w1[512 * c : 512 * (c + 1), P * b : P * (b + 1)].rearrange("(p j) w -> p j w", j=4),
                 )
+            w_wide_raw[b] = wr
+
+        def interleave_w1_wide(b):
             grouped = two.tile([P, PASSES, P, 4], BF16, align_bytes=64, name="w_wide_grouped")
-            nc.scalar.copy(out=grouped[:], in_=wr[:].rearrange("p c j w -> p c w j"))
+            nc.scalar.copy(out=grouped[:], in_=w_wide_raw[b][:].rearrange("p c j w -> p c w j"))
             w_wide[b] = grouped
 
         def quantize_w1_wide(b):
@@ -295,35 +301,42 @@ def tile_picked_gcn_mlp_none_sub_l_kernel(tc, xT, w1, w2, gate, pos1, pos2, pos3
             prods = []
             for d in range(D):
                 prods.append(gather(b, d, 0, V))
+                if d == 0 and b > 0:
+                    sum_block(b - 1, last_prods)
                 if b == 0:
                     if d < PASSES:
                         prepare_w1(1, d, True)
                         project(1, d)
-                    if d == PASSES:
-                        bring_out(1)
-                    if d == 5:
-                        load_w1_wide(2)
+                        if d == PASSES - 1:
+                            bring_out(1)
+                            load_w1_wide(3)
+                    else:
+                        for c in range(2 * (d - PASSES), 2 * (d - PASSES) + 2):
+                            prepare_w1(2, c, True)
+                            project(2, c)
+                        if d == D - 1:
+                            bring_out(2)
+                            interleave_w1_wide(3)
+                            load_w1_wide(4)
                 else:
-                    if d == 0:
-                        sum_block(b - 1, last_prods)
-                    if d == 1:
-                        quantize_w1_wide(b + 1)
+                    if d == 2 and b + 2 < BLOCKS:
+                        quantize_w1_wide(b + 2)
                         for c in range(PASSES):
-                            project(b + 1, c)
-                        bring_out(b + 1)
-                    if d == 2:
-                        if b == 1:
-                            load_w2()
-                        if b + 2 < BLOCKS:
-                            load_w1_wide(b + 2)
-                    if d == 4:
-                        if b == 2:
-                            quantize_w2()
-                        if b == 4:
-                            grouped = keep.tile([P, V, 4], BF16, align_bytes=64, name="z_grouped_0")
-                            for v0 in (0, 2):
-                                turn_back(0, v0, 2, grouped[:, P * v0 : P * (v0 + 2), :].bitcast(F32), nc.scalar.copy)
-                            grouped_half[0] = grouped
+                            project(b + 2, c)
+                        bring_out(b + 2)
+                        if b + 3 < BLOCKS:
+                            interleave_w1_wide(b + 3)
+                        if b + 4 < BLOCKS:
+                            load_w1_wide(b + 4)
+                    if d == 3 and b == 1:
+                        load_w2()
+                    if d == 4 and b == 2:
+                        quantize_w2()
+                    if d == 4 and b == 4:
+                        grouped = keep.tile([P, V, 4], BF16, align_bytes=64, name="z_grouped_0")
+                        for v0 in (0, 2):
+                            turn_back(0, v0, 2, grouped[:, P * v0 : P * (v0 + 2), :].bitcast(F32), nc.scalar.copy)
+                        grouped_half[0] = grouped
                     if d == 0 and b == 5:
                         quantize_z(0, 0, VT, grouped_half[0][:].rearrange("p n j -> p (n j)"))
             last_prods = prods

@@ -28,7 +28,7 @@ def tile_picked_gcn_mlp_none_sub_l_kernel(tc, xT, w1, w2, gate, pos1, pos2, pos3
         raw = ctx.enter_context(tc.tile_pool(name="raw", bufs=3))
         ring = ctx.enter_context(tc.tile_pool(name="ring", bufs=4))
         two = ctx.enter_context(tc.tile_pool(name="two", bufs=2))
-        wpool = ctx.enter_context(tc.tile_pool(name="wpool", bufs=8))
+        wpool = ctx.enter_context(tc.tile_pool(name="wpool", bufs=4))
         hbank = ctx.enter_context(tc.psum_pool(name="hbank", bufs=4))
         zbank = ctx.enter_context(tc.psum_pool(name="zbank", bufs=2))
 
@@ -45,12 +45,13 @@ def tile_picked_gcn_mlp_none_sub_l_kernel(tc, xT, w1, w2, gate, pos1, pos2, pos3
         w_raw = {}
 
         def load_w1(b):
-            for c in range(PASSES):
-                wr = wpool.tile([P, 4, P], F32)
-                nc.sync.dma_start(
-                    out=wr[:],
-                    in_=w1[512 * c : 512 * (c + 1), P * b : P * (b + 1)].rearrange("(p j) w -> p j w", j=4),
-                )
+            for c in range(0, PASSES, 2):
+                wr = wpool.tile([P, 2, 4, P], F32)
+                for k in range(2):
+                    nc.sync.dma_start(
+                        out=wr[:, k, :, :],
+                        in_=w1[512 * (c + k) : 512 * (c + k + 1), P * b : P * (b + 1)].rearrange("(p j) w -> p j w", j=4),
+                    )
                 w_raw[b, c] = wr
 
         load_w1(0)
@@ -64,7 +65,7 @@ def tile_picked_gcn_mlp_none_sub_l_kernel(tc, xT, w1, w2, gate, pos1, pos2, pos3
                 x_raw.append([(xr, 0)])
             else:
                 parts = []
-                for lo, n in ((0, 512), (512, 256), (768, 256)):
+                for lo, n in ((0, 512), (512, 384), (896, 128)):
                     xh = raw.tile([P, 4, n], F32, name="half_raw")
                     nc.sync.dma_start(out=xh[:], in_=rows[:, lo : lo + n].rearrange("(p j) t -> p j t", j=4))
                     parts.append((xh, lo))
@@ -84,11 +85,13 @@ def tile_picked_gcn_mlp_none_sub_l_kernel(tc, xT, w1, w2, gate, pos1, pos2, pos3
                 scales = ring.tile([P, PASSES, P], U8, align_bytes=64, name="w_scales")
                 w_codes[b] = (codes, scales)
             codes, scales = w_codes[b]
-            grouped = wpool.tile([P, P, 4], BF16, align_bytes=64, name="w_grouped")
+            grouped = wpool.tile([P, 2, P, 4], BF16, align_bytes=64, name="w_grouped")
             copy = nc.scalar.copy if on_scalar else nc.vector.tensor_copy
-            copy(out=grouped[:], in_=w_raw[b, c][:].rearrange("p j w -> p w j"))
+            copy(out=grouped[:], in_=w_raw[b, c][:].rearrange("p k j w -> p k w j"))
             nc.vector.quantize_mx(
-                out=codes[:, c, :].bitcast(X4), scales=scales[:, c, :], in_=grouped[:].rearrange("p w j -> p (w j)")
+                out=codes[:, c : c + 2, :].rearrange("p k w -> p (k w)").bitcast(X4),
+                scales=scales[:, c : c + 2, :].rearrange("p k w -> p (k w)"),
+                in_=grouped[:].rearrange("p k w j -> p (k w j)"),
             )
 
         w_wide = {}
@@ -137,16 +140,11 @@ def tile_picked_gcn_mlp_none_sub_l_kernel(tc, xT, w1, w2, gate, pos1, pos2, pos3
         def project(b, c):
             if c == 0:
                 h_banks[b] = []
-                for lo, n in ((0, 512), (512, 256), (768, 256)) if b == 0 else ((0, 512), (512, 512)):
+                for lo, n in ((0, 512), (512, 256), (768, 128), (896, 128)) if b == 0 else ((0, 512), (512, 512)):
                     bank = hbank.tile([P, n], F32, name="h")
                     h_banks[b].append((bank, lo, n))
             for bank, lo, n in h_banks[b]:
-                if b > 0 or c < PASSES - 1 or lo < 768:
-                    project_group(b, c, bank, lo, n)
-
-        def project_last_quarter():
-            bank, lo, n = h_banks[0][2]
-            project_group(0, PASSES - 1, bank, lo, n)
+                project_group(b, c, bank, lo, n)
 
         x_codes = keep.tile([P, PASSES, T], U32, align_bytes=64)
         x_scales = keep.tile([P, PASSES, T], U8, align_bytes=64)
@@ -170,11 +168,7 @@ def tile_picked_gcn_mlp_none_sub_l_kernel(tc, xT, w1, w2, gate, pos1, pos2, pos3
                 in_=x_grouped[c, lo].rearrange("p t j -> p (t j)"),
             )
 
-        def prepare_x(c, lo, n, on_scalar):
-            interleave_x(c, lo, n, on_scalar)
-            quantize_x(c, lo, n)
-
-        for c in range(PASSES):
+        for c in range(0, PASSES, 2):
             prepare_w1(0, c, False)
         gate_cols = zbank.tile([P, VT, P], F32, tag="zz")
         for v in range(VT):
@@ -195,27 +189,35 @@ def tile_picked_gcn_mlp_none_sub_l_kernel(tc, xT, w1, w2, gate, pos1, pos2, pos3
 
         for c in range(3):
             interleave_x(c, 512, 512, True)
-            prepare_x(c, 0, 512, False)
+            interleave_x(c, 0, 512, False)
             if c > 0:
                 quantize_x(c - 1, 512, 512)
                 project(0, c - 1)
-        interleave_x(3, 0, 256, True)
-        prepare_x(3, 256, 256, False)
-        quantize_x(2, 512, 512)
-        project(0, 2)
-        prepare_x(3, 512, 256, False)
-        quantize_x(3, 0, 256)
-        project(0, 3)
+            quantize_x(c, 0, 512)
         first = raw.tile([P, T], F32, name="h_rows")
         h_tiles[0] = first
-        nc.scalar.copy(out=first[:, 0:512], in_=h_banks[0][0][0][:])
-        interleave_x(3, 768, 128, False)
-        interleave_x(3, 896, 128, True)
-        nc.vector.tensor_copy(out=first[:, 512:768], in_=h_banks[0][1][0][:])
+
+        def finish_first(g):
+            bank, lo, n = h_banks[0][g]
+            project_group(0, PASSES - 1, bank, lo, n)
+            nc.scalar.copy(out=first[:, lo : lo + n], in_=bank[:])
+
+        interleave_x(3, 0, 256, True)
+        interleave_x(3, 256, 256, False)
+        quantize_x(2, 512, 512)
+        project(0, 2)
+        quantize_x(3, 256, 256)
+        interleave_x(3, 768, 128, True)
+        interleave_x(3, 512, 256, False)
+        quantize_x(3, 0, 256)
+        finish_first(0)
+        quantize_x(3, 512, 256)
+        finish_first(1)
+        interleave_x(3, 896, 128, False)
         quantize_x(3, 768, 128)
+        finish_first(2)
         quantize_x(3, 896, 128)
-        project_last_quarter()
-        nc.scalar.copy(out=first[:, 768:1024], in_=h_banks[0][2][0][:])
+        finish_first(3)
 
         def bring_out(b):
             h = raw.tile([P, T], F32, name="h_rows")
@@ -304,20 +306,18 @@ def tile_picked_gcn_mlp_none_sub_l_kernel(tc, xT, w1, w2, gate, pos1, pos2, pos3
                 if d == 0 and b > 0:
                     sum_block(b - 1, last_prods)
                 if b == 0:
-                    if d < PASSES:
-                        prepare_w1(1, d, True)
-                        project(1, d)
-                        if d == PASSES - 1:
-                            bring_out(1)
-                            load_w1_wide(3)
-                    else:
-                        for c in range(2 * (d - PASSES), 2 * (d - PASSES) + 2):
-                            prepare_w1(2, c, True)
-                            project(2, c)
-                        if d == D - 1:
-                            bring_out(2)
-                            interleave_w1_wide(3)
-                            load_w1_wide(4)
+                    if d in (1, 2, 4, 5):
+                        ahead, c = {1: (1, 0), 2: (1, 2), 4: (2, 0), 5: (2, 2)}[d]
+                        prepare_w1(ahead, c, True)
+                        project(ahead, c)
+                        project(ahead, c + 1)
+                        if c > 0:
+                            bring_out(ahead)
+                    if d == 2:
+                        load_w1_wide(3)
+                    if d == 5:
+                        interleave_w1_wide(3)
+                        load_w1_wide(4)
                 else:
                     if d == 2 and b + 2 < BLOCKS:
                         quantize_w1_wide(b + 2)
@@ -382,4 +382,4 @@ def tile_picked_gcn_mlp_none_sub_l_kernel(tc, xT, w1, w2, gate, pos1, pos2, pos3
                     )
             res = two.tile([P, 384], F32, name="result")
             nc.scalar.copy(out=res[:, 0:n], in_=acc[:])
-            nc.sync.dma_start(out=out[:, lo : lo + n], in_=res[:, 0:n])
+            nc.scalar.dma_start(out=out[:, lo : lo + n], in_=res[:, 0:n])

from contextlib import ExitStack

import concourse.mybir as mybir
from concourse.masks import make_identity

K, T, D, V, H, N = 2048, 1024, 6, 512, 1024, 128
FLOPS = 2 * K * T * H + 2 * H * V * N

F32 = mybir.dt.float32
BF16 = mybir.dt.bfloat16
U32 = mybir.dt.uint32
U16 = mybir.dt.uint16
U8 = mybir.dt.uint8
X4 = mybir.dt.float8_e4m3fn_x4
MULT = mybir.AluOpType.mult

P = 128
PASSES = K // 512
BLOCKS = H // P
VT = V // P


def tile_picked_gcn_mlp_none_sub_l_kernel(tc, xT, w1, w2, gate, pos1, pos2, pos3, pos4, pos5, pos6, out):
    nc = tc.nc
    with ExitStack() as ctx:
        lists_pool = ctx.enter_context(tc.tile_pool(name="lists", bufs=1))
        keep = ctx.enter_context(tc.tile_pool(name="keep", bufs=1))
        raw = ctx.enter_context(tc.tile_pool(name="raw", bufs=3))
        ring = ctx.enter_context(tc.tile_pool(name="ring", bufs=4))
        two = ctx.enter_context(tc.tile_pool(name="two", bufs=2))
        wpool = ctx.enter_context(tc.tile_pool(name="wpool", bufs=4))
        hbank = ctx.enter_context(tc.psum_pool(name="hbank", bufs=4))
        zbank = ctx.enter_context(tc.psum_pool(name="zbank", bufs=2))

        lists = []
        for d in range(D):
            offs = lists_pool.tile([P, V // 16], U16, name=f"pos_{d}")
            lists.append(offs)

        gate_rows = keep.tile([P, V], F32)
        nc.vector.memset(gate_rows[:], 0.0)
        ident = keep.tile([P, P], F32)
        make_identity(nc, ident[:])

        w_raw = {}

        def load_w1(b):
            for c in range(0, PASSES, 2):
                wr = wpool.tile([P, 2, 4, P], F32)
                for k in range(2):
                    nc.sync.dma_start(
                        out=wr[:, k, :, :],
                        in_=w1[512 * (c + k) : 512 * (c + k + 1), P * b : P * (b + 1)].rearrange("(p j) w -> p j w", j=4),
                    )
                w_raw[b, c] = wr

        load_w1(0)
        nc.sync.dma_start(out=gate_rows[0:D, :], in_=gate[:, 0, :])
        x_raw = []
        for c in range(PASSES):
            rows = xT[512 * c : 512 * (c + 1), :]
            if c < PASSES - 1:
                xr = raw.tile([P, 4, T], F32)
                nc.sync.dma_start(out=xr[:], in_=rows.rearrange("(p j) t -> p j t", j=4))
                x_raw.append([(xr, 0)])
            else:
                parts = []
                for lo, n in ((0, 512), (512, 384), (896, 128)):
                    xh = raw.tile([P, 4, n], F32, name="half_raw")
                    nc.sync.dma_start(out=xh[:], in_=rows[:, lo : lo + n].rearrange("(p j) t -> p j t", j=4))
                    parts.append((xh, lo))
                x_raw.append(parts)
            if c == 1:
                for offs, src in zip(lists, (pos1, pos2, pos3, pos4, pos5, pos6)):
                    nc.sync.dma_start(out=offs[:], in_=src)

        load_w1(1)
        load_w1(2)

        w_codes = {}

        def prepare_w1(b, c, on_scalar):
            if c == 0:
                codes = ring.tile([P, PASSES, P], U32, align_bytes=64, name="w_codes")
                scales = ring.tile([P, PASSES, P], U8, align_bytes=64, name="w_scales")
                w_codes[b] = (codes, scales)
            codes, scales = w_codes[b]
            grouped = wpool.tile([P, 2, P, 4], BF16, align_bytes=64, name="w_grouped")
            copy = nc.scalar.copy if on_scalar else nc.vector.tensor_copy
            copy(out=grouped[:], in_=w_raw[b, c][:].rearrange("p k j w -> p k w j"))
            nc.vector.quantize_mx(
                out=codes[:, c : c + 2, :].rearrange("p k w -> p (k w)").bitcast(X4),
                scales=scales[:, c : c + 2, :].rearrange("p k w -> p (k w)"),
                in_=grouped[:].rearrange("p k w j -> p (k w j)"),
            )

        w_wide = {}

        w_wide_raw = {}

        def load_w1_wide(b):
            wr = raw.tile([P, PASSES, 4, P], F32, name="half_raw")
            for c in range(PASSES):
                nc.sync.dma_start(
                    out=wr[:, c, :, :],
                    in_=w1[512 * c : 512 * (c + 1), P * b : P * (b + 1)].rearrange("(p j) w -> p j w", j=4),
                )
            w_wide_raw[b] = wr

        def interleave_w1_wide(b):
            grouped = two.tile([P, PASSES, P, 4], BF16, align_bytes=64, name="w_wide_grouped")
            nc.scalar.copy(out=grouped[:], in_=w_wide_raw[b][:].rearrange("p c j w -> p c w j"))
            w_wide[b] = grouped

        def quantize_w1_wide(b):
            codes = ring.tile([P, PASSES, P], U32, align_bytes=64, name="w_codes")
            scales = ring.tile([P, PASSES, P], U8, align_bytes=64, name="w_scales")
            w_codes[b] = (codes, scales)
            nc.vector.quantize_mx(
                out=codes[:].rearrange("p c w -> p (c w)").bitcast(X4),
                scales=scales[:].rearrange("p c w -> p (c w)"),
                in_=w_wide[b][:].rearrange("p c w j -> p (c w j)"),
            )

        h_tiles = {}
        h_banks = {}

        def project_group(b, c, bank, lo, n):
            codes, scales = w_codes[b]
            nc.tensor.matmul_mx(
                out=bank[:],
                lhsT=codes[:, c, :].bitcast(X4),
                lhsT_scale=scales[:, c, :],
                rhs=x_codes[:, c, lo : lo + n].bitcast(X4),
                rhs_scale=x_scales[:, c, lo : lo + n],
                start=(c == 0),
                stop=(c == PASSES - 1),
            )

        def project(b, c):
            if c == 0:
                h_banks[b] = []
                for lo, n in ((0, 512), (512, 256), (768, 128), (896, 128)) if b == 0 else ((0, 512), (512, 512)):
                    bank = hbank.tile([P, n], F32, name="h")
                    h_banks[b].append((bank, lo, n))
            for bank, lo, n in h_banks[b]:
                project_group(b, c, bank, lo, n)

        x_codes = keep.tile([P, PASSES, T], U32, align_bytes=64)
        x_scales = keep.tile([P, PASSES, T], U8, align_bytes=64)

        x_grouped = {}

        def interleave_x(c, lo, n, on_scalar):
            for tile, base in x_raw[c]:
                if base <= lo < base + tile.shape[2]:
                    src = tile[:, :, lo - base : lo - base + n]
            grouped = ring.tile([P, 512, 4], BF16, align_bytes=64, name="x_grouped")
            view = grouped[:, 0:n, :]
            copy = nc.scalar.copy if on_scalar else nc.vector.tensor_copy
            copy(out=view, in_=src.rearrange("p j t -> p t j"))
            x_grouped[c, lo] = view

        def quantize_x(c, lo, n):
            nc.vector.quantize_mx(
                out=x_codes[:, c, lo : lo + n].bitcast(X4),
                scales=x_scales[:, c, lo : lo + n],
                in_=x_grouped[c, lo].rearrange("p t j -> p (t j)"),
            )

        for c in range(0, PASSES, 2):
            prepare_w1(0, c, False)
        gate_cols = zbank.tile([P, VT, P], F32, tag="zz")
        for v in range(VT):
            nc.tensor.transpose(gate_cols[:, v, :], gate_rows[:, P * v : P * (v + 1)], ident[:])
        gate_t = keep.tile([P, VT, 8], F32)
        nc.vector.tensor_copy(out=gate_t[:, :, 0:D], in_=gate_cols[:, :, 0:D])
        gates = []
        for d in range(D):
            gb = zbank.tile([P, V], F32, tag=("zt", "zz")[d % 2])
            for v in range(VT):
                nc.tensor.transpose(gb[:, P * v : P * (v + 1)], gate_t[:, v, d : d + 1].to_broadcast([P, P]), ident[:])
            gd = keep.tile([P, V], F32, name=f"gate_{d}")
            if d % 2 == 0:
                nc.scalar.copy(out=gd[:], in_=gb[:])
            else:
                nc.vector.tensor_copy(out=gd[:], in_=gb[:])
            gates.append(gd)

        for c in range(3):
            interleave_x(c, 512, 512, True)
            interleave_x(c, 0, 512, False)
            if c > 0:
                quantize_x(c - 1, 512, 512)
                project(0, c - 1)
            quantize_x(c, 0, 512)
        first = raw.tile([P, T], F32, name="h_rows")
        h_tiles[0] = first

        def finish_first(g):
            bank, lo, n = h_banks[0][g]
            project_group(0, PASSES - 1, bank, lo, n)
            nc.scalar.copy(out=first[:, lo : lo + n], in_=bank[:])

        interleave_x(3, 0, 256, True)
        interleave_x(3, 256, 256, False)
        quantize_x(2, 512, 512)
        project(0, 2)
        quantize_x(3, 256, 256)
        interleave_x(3, 768, 128, True)
        interleave_x(3, 512, 256, False)
        quantize_x(3, 0, 256)
        finish_first(0)
        quantize_x(3, 512, 256)
        finish_first(1)
        interleave_x(3, 896, 128, False)
        quantize_x(3, 768, 128)
        finish_first(2)
        quantize_x(3, 896, 128)
        finish_first(3)

        def bring_out(b):
            h = raw.tile([P, T], F32, name="h_rows")
            h_tiles[b] = h
            for bank, lo, n in h_banks[b]:
                nc.scalar.copy(out=h[:, lo : lo + n], in_=bank[:])

        def gather(b, d, lo, n):
            prod = two.tile([P, V], F32, name=f"prod_{d}")
            cols = slice(lo, lo + n)
            if n == V:
                offs = lists[d][:]
            else:
                offs = lists[d][:, lo // 16 : (lo + n) // 16]
            nc.vector.tensor_tensor(prod[:, 0:n], h_tiles[b][:].indirect(offs), gates[d][:, cols], MULT)
            return prod

        def add_transposed(bank_cols, prod_cols, d):
            nc.tensor.matmul(bank_cols, lhsT=prod_cols, rhs=ident[:], is_transpose=True, start=(d == 0), stop=(d == D - 1))

        z_half = {}

        def z_rows(b):
            if b // 4 not in z_half:
                zb = two.tile([P, VT, 512], BF16, align_bytes=64, name="z_rows")
                z_half[b // 4] = zb
            return z_half[b // 4]

        def sum_block(b, prods):
            zt = zbank.tile([P, VT, P], F32, tag="zt")
            for v in range(VT):
                for d in range(D):
                    add_transposed(zt[:, v, :], prods[d][:, P * v : P * (v + 1)], d)
            q = b % 4
            nc.scalar.copy(out=z_rows(b)[:, :, P * q : P * (q + 1)], in_=zt[:])

        z_codes = keep.tile([P, 2, V], U32, align_bytes=64)
        z_scales = keep.tile([P, 2, V], U8, align_bytes=64)

        def turn_back(half, v0, nv, grouped, copy):
            words = z_half[half][:].rearrange("p v i -> p (v i)").bitcast(F32)
            zz = zbank.tile([P, 2, 2, P], F32, tag="zz")
            for v in range(nv):
                for u in range(2):
                    base = 256 * (v0 + v)
                    nc.tensor.transpose(zz[:, v, u, :], words[:, base + u : base + 256 : 2], ident[:])
            copy(
                out=grouped.rearrange("p (v n) w -> p v n w", v=nv),
                in_=zz[:, 0:nv, :, :].rearrange("p v u n -> p v n u"),
            )

        def quantize_z(half, v0, nv, grouped_bf):
            cols = slice(P * v0, P * (v0 + nv))
            nc.vector.quantize_mx(
                out=z_codes[:, half, cols].bitcast(X4),
                scales=z_scales[:, half, cols],
                in_=grouped_bf,
            )

        w2_state = {}

        def load_w2():
            wr = keep.tile([P, 2, 4, P], F32, name="w2_raw")
            for g in range(2):
                nc.sync.dma_start(out=wr[:, g, :, :], in_=w2[512 * g : 512 * (g + 1), :].rearrange("(p j) m -> p j m", j=4))
            grouped = keep.tile([P, 2, P, 4], BF16, align_bytes=64, name="w2_grouped")
            nc.scalar.copy(out=grouped[:], in_=wr[:].rearrange("p g j m -> p g m j"))
            w2_state["grouped"] = grouped

        w2_codes = keep.tile([P, 2, P], U32, align_bytes=64)
        w2_scales = keep.tile([P, 2, P], U8, align_bytes=64)

        def quantize_w2():
            nc.vector.quantize_mx(
                out=w2_codes[:].rearrange("p g m -> p (g m)").bitcast(X4),
                scales=w2_scales[:].rearrange("p g m -> p (g m)"),
                in_=w2_state["grouped"][:].rearrange("p g m j -> p (g m j)"),
            )

        grouped_half = {}
        last_prods = None
        for b in range(BLOCKS - 1):
            prods = []
            for d in range(D):
                prods.append(gather(b, d, 0, V))
                if d == 0 and b > 0:
                    sum_block(b - 1, last_prods)
                if b == 0:
                    if d in (1, 2, 4, 5):
                        ahead, c = {1: (1, 0), 2: (1, 2), 4: (2, 0), 5: (2, 2)}[d]
                        prepare_w1(ahead, c, True)
                        project(ahead, c)
                        project(ahead, c + 1)
                        if c > 0:
                            bring_out(ahead)
                    if d == 2:
                        load_w1_wide(3)
                    if d == 5:
                        interleave_w1_wide(3)
                        load_w1_wide(4)
                else:
                    if d == 2 and b + 2 < BLOCKS:
                        quantize_w1_wide(b + 2)
                        for c in range(PASSES):
                            project(b + 2, c)
                        bring_out(b + 2)
                        if b + 3 < BLOCKS:
                            interleave_w1_wide(b + 3)
                        if b + 4 < BLOCKS:
                            load_w1_wide(b + 4)
                    if d == 3 and b == 1:
                        load_w2()
                    if d == 4 and b == 2:
                        quantize_w2()
                    if d == 4 and b == 4:
                        grouped = keep.tile([P, V, 4], BF16, align_bytes=64, name="z_grouped_0")
                        for v0 in (0, 2):
                            turn_back(0, v0, 2, grouped[:, P * v0 : P * (v0 + 2), :].bitcast(F32), nc.scalar.copy)
                        grouped_half[0] = grouped
                    if d == 0 and b == 5:
                        quantize_z(0, 0, VT, grouped_half[0][:].rearrange("p n j -> p (n j)"))
            last_prods = prods

        b = BLOCKS - 1
        grouped = keep.tile([P, V, 4], BF16, align_bytes=64, name="z_grouped_1")
        zb = z_rows(b)
        zts = []
        for v in range(VT):
            zt = hbank.tile([P, P], F32, name="h")
            zts.append(zt)
        for d in range(3):
            prod = gather(b, d, 0, V)
            for v in range(VT):
                add_transposed(zts[v][:], prod[:, P * v : P * (v + 1)], d)
            if d == 0:
                sum_block(b - 1, last_prods)
        for lo, n in ((0, 384), (384, 128)):
            v0, nv = lo // P, n // P
            for d in range(3, D):
                prod = gather(b, d, lo, n)
                for v in range(nv):
                    add_transposed(zts[v0 + v][:], prod[:, P * v : P * (v + 1)], d)
            for v in range(v0, v0 + nv):
                copy = nc.scalar.copy if lo == 0 else nc.vector.tensor_copy
                copy(out=zb[:, v, 384:512], in_=zts[v][:])
            for v in range(0, nv, 2):
                turn_back(1, v0 + v, min(2, nv - v), grouped[:, P * (v0 + v) : P * (v0 + min(v + 2, nv)), :].bitcast(F32), nc.scalar.copy)
        for lo, n in ((0, 384), (384, 128)):
            acc = zbank.tile([P, n], F32, tag="zt")
            for start, width in ((0, 256), (256, 128)) if lo == 0 else ((384, 128),):
                cols = slice(start, start + width)
                quantize_z(1, start // P, width // P, grouped[:, cols, :].rearrange("p n j -> p (n j)"))
                for g in range(2):
                    nc.tensor.matmul_mx(
                        out=acc[:, start - lo : start - lo + width],
                        lhsT=w2_codes[:, g, :].bitcast(X4),
                        lhsT_scale=w2_scales[:, g, :],
                        rhs=z_codes[:, g, cols].bitcast(X4),
                        rhs_scale=z_scales[:, g, cols],
                        start=(g == 0),
                        stop=(g == 1),
                    )
            res = two.tile([P, 384], F32, name="result")
            nc.scalar.copy(out=res[:, 0:n], in_=acc[:])
            nc.scalar.dma_start(out=out[:, lo : lo + n], in_=res[:, 0:n])
